import numpy as np
import ml_dtypes


def mxq(x, axis, fmt="e4m3"):
    dtype, down = {"e4m3": (ml_dtypes.float8_e4m3fn, 7), "e5m2": (ml_dtypes.float8_e5m2, 14)}[fmt]
    v = np.moveaxis(np.asarray(x, np.float32).astype(ml_dtypes.bfloat16).astype(np.float64), axis, -1)
    blocks = v.reshape(v.shape[:-1] + (-1, 32))
    amax = np.abs(blocks).max(-1, keepdims=True)
    byte = np.maximum(np.where(amax > 0, np.frexp(amax)[1] - 1 + 127, 0) - down, 1)
    scale = np.exp2(byte - 127.0)
    codes = (blocks / scale).astype(np.float32).astype(dtype).astype(np.float64)
    return np.moveaxis((codes * scale).reshape(v.shape), -1, axis)


WIDE = False


def mx_kscale(k):
    if not WIDE:
        return np.ones(k)
    levels = np.array([10, -10, 5, -5, 0])
    if k % 512:
        return np.exp2(np.random.permutation(np.resize(levels, k // 32))).repeat(32)
    a = np.empty((k // 512, 16))
    for p in range(k // 512):
        a[p, :8] = np.random.permutation(np.resize(levels, 8))
        for g in range(8):
            far = levels[np.abs(levels - a[p, g]) >= 10]
            a[p, g + 8] = far[np.random.randint(len(far))]
    return np.exp2(a.ravel()).repeat(32)


def f64(x):
    return np.asarray(x).astype(np.float64)


def striped(idx):
    return np.tile(idx.reshape(-1, 16).T, (8, 1)).astype(np.uint16)


def unstriped(offs):
    return offs[:16].T.reshape(-1).astype(np.int64)


E2M1 = np.array([0.0, 0.5, 1.0, 1.5, 2.0, 3.0, 4.0, 6.0, -0.0, -0.5, -1.0, -1.5, -2.0, -3.0, -4.0, -6.0])


def pack_weight(w, fmt):
    k, n = w.shape
    w = f64(np.asarray(w, np.float32).astype(ml_dtypes.bfloat16)).reshape(k // 32, 32, n)
    amax = np.abs(w).max(1)
    if fmt == "e4m3":
        byte = np.frexp(amax)[1] - 1 + 127 - 7
    else:
        mant, ex = np.frexp(amax / 6.0)
        byte = np.where(mant > 0.5, ex, ex - 1) + 127
    byte = np.clip(np.where(amax > 0, byte, 1), 1, 254)
    scaled = (w * np.exp2(127.0 - byte)[:, None, :]).reshape(k, n).astype(np.float32)
    by_word = np.ascontiguousarray(scaled.reshape(k // 512, 128, 4, n).transpose(0, 1, 3, 2))
    if fmt == "e4m3":
        words = by_word.astype(ml_dtypes.float8_e4m3fn).view(np.uint8)
    else:
        c = by_word.astype(ml_dtypes.float4_e2m1fn).view(np.uint8) & 0xF
        words = (c[..., 0::2] | (c[..., 1::2] << 4)).reshape(k // 512, 128, 2 * n)
    return np.ascontiguousarray(words), np.ascontiguousarray(byte.astype(np.uint8).reshape(k // 512, 16, n))


def unpack_weight(words, scales, fmt):
    g, _, n = scales.shape
    words = np.ascontiguousarray(words).reshape(g, 128, n, -1)
    if fmt == "e4m3":
        vals = words.view(ml_dtypes.float8_e4m3fn).astype(np.float64)
    else:
        nib = np.empty((g, 128, n, 4), np.uint8)
        nib[..., 0::2] = words & 0xF
        nib[..., 1::2] = words >> 4
        vals = E2M1[nib]
    vals = vals * np.repeat(np.exp2(scales.astype(np.float64) - 127.0), 8, axis=1)[..., None]
    return vals.transpose(0, 1, 3, 2).reshape(g * 512, n)


def gelu(v):
    return 0.5 * v * (1.0 + np.tanh(np.sqrt(2.0 / np.pi) * (v + 0.044715 * v**3)))


K, H, N, T, S, M, TB, P = 512, 1024, 512, 4096, 1024, 1024, 2048, 512

def setup_inputs():
    n = np.random.standard_normal
    s = mx_kscale(K)[:, None]
    s2 = mx_kscale(M)[:, None]
    u = mx_kscale(H)[:, None]
    tab_words, tab_scales = pack_weight(n((K, T)) * s, "e4m3")
    tab2_words, tab2_scales = pack_weight(n((M, TB)) * s2, "e4m3")
    w1 = (1.6 * n((K, H)) / np.sqrt(K) / s).astype(np.float32)
    w2_words, w2_scales = pack_weight(1.6 * n((K, H)) / np.sqrt(K) / s, "e2m1")
    gain = (np.exp(0.4 * n(H)) * u[:, 0]).astype(np.float32)
    w3 = (1.4 * n((H, N)) / np.sqrt(H) / u).astype(np.float32)
    w4 = (1.2 * n((M, N)) / np.sqrt(M) / s2).astype(np.float32)
    w5_words, w5_scales = pack_weight(1.2 * n((M, N)) / np.sqrt(M) / s2, "e4m3")
    low = (-1.0 + 0.4 * n(N)).astype(np.float32)
    return dict(tab_words=tab_words, tab_scales=tab_scales, offs=striped(np.random.permutation(T)[:S]),
                tab2_words=tab2_words, tab2_scales=tab2_scales, offs2=striped(np.random.permutation(TB)[:P]),
                pos1=striped(np.random.permutation(S)[:P]), w1=w1, w2_words=w2_words, w2_scales=w2_scales,
                gain=gain, w3=w3, w4=w4, w5_words=w5_words, w5_scales=w5_scales, low=low)

def reference(tab_words, tab_scales, offs, tab2_words, tab2_scales, offs2, pos1, w1, w2_words, w2_scales,
              gain, w3, w4, w5_words, w5_scales, low):
    v = unpack_weight(tab_words, tab_scales, "e4m3")[:, unstriped(offs)]
    v2 = unpack_weight(tab2_words, tab2_scales, "e4m3")[:, unstriped(offs2)]
    d1 = mxq(f64(w1), 0, "e4m3").T @ v
    d2 = unpack_weight(w2_words, w2_scales, "e2m1").T @ v
    h = f64(gain)[:, None] * np.tanh(np.minimum(d1, d2))
    y = mxq(f64(w3), 0, "e4m3").T @ mxq(h, 0, "e4m3")
    cap = mxq(f64(w4), 0, "e4m3").T @ v2
    base = unpack_weight(w5_words, w5_scales, "e4m3").T @ v2
    return np.maximum(np.minimum(y[:, unstriped(pos1)], cap), base + f64(low)[:, None])

@@ -1,0 +1,269 @@
+from contextlib import ExitStack
+
+import concourse.mybir as mybir
+
+K, H, N, T, S, M, TB, PICK = 512, 1024, 512, 4096, 1024, 1024, 2048, 512
+FLOPS = 2 * (2 * K * H * S + H * N * S + 2 * M * N * PICK)
+
+F32 = mybir.dt.float32
+BF16 = mybir.dt.bfloat16
+I32 = mybir.dt.int32
+U32 = mybir.dt.uint32
+U16 = mybir.dt.uint16
+U8 = mybir.dt.uint8
+FP8X4 = mybir.dt.float8_e4m3fn_x4
+FP4X4 = mybir.dt.float4_e2m1fn_x4
+ALU = mybir.AluOpType
+ACT = mybir.ActivationFunctionType
+
+P = 128
+PACK = 4
+PASS = P * PACK
+BANK = 512
+CHUNK = BANK // PACK
+PAIR = 2 * CHUNK
+
+
+def tile_list_crystal_deposit_grading_kernel(
+    tc, tab_words, tab_scales, offs, tab2_words, tab2_scales, offs2, pos1, w1, w2_words, w2_scales,
+    gain, w3, w4, w5_words, w5_scales, low, out,
+):
+    nc = tc.nc
+    with ExitStack() as ctx:
+        keep = ctx.enter_context(tc.tile_pool(name="keep", bufs=1))
+        ring = ctx.enter_context(tc.tile_pool(name="ring", bufs=3))
+        psum = ctx.enter_context(tc.psum_pool(name="psum", bufs=1))
+
+        def kept(name, width, dtype):
+            return keep.tile([P, width], dtype, name=name, align_bytes=64)
+
+        def words_of(dram):
+            return dram.rearrange("p n t -> p (n t)").bitcast(I32)
+
+        def load_scales(queue, plane, dram):
+            passes = dram.shape[0]
+            for q in range(4):
+                rows = dram[:, 4 * q : 4 * q + 4, :] if passes > 1 else dram[0, 4 * q : 4 * q + 4, :]
+                queue.dma_start(out=plane[32 * q : 32 * q + 4 * passes, :].bitcast(I32), in_=rows.bitcast(I32))
+
+        def load_block(name, w, a, c0, width):
+            raw = keep.tile([P, PACK, width], F32, name=name)
+            rows = w[a * PASS : (a + 1) * PASS, c0 : c0 + width]
+            nc.sync.dma_start(out=raw[:], in_=rows.rearrange("(p j) c -> p j c", j=PACK))
+            return raw
+
+        def load_rows(name, w, a, c0):
+            raw = load_block(name, w, a, c0, BANK)
+            return [raw[:, :, 0:PAIR], raw[:, :, PAIR:BANK]]
+
+        def load_halves(name, w, a, c0):
+            return [load_block(f"{name}_{u}", w, a, c0 + u * PAIR, PAIR)[:] for u in range(2)]
+
+        offs_sb = keep.tile([P, S // 16], U16, name="offs_sb")
+        offs2_sb = keep.tile([P, PICK // 16], U16, name="offs2_sb")
+        pos1_sb = keep.tile([P, PICK // 16], U16, name="pos1_sb")
+        tabw = kept("tabw", T, U32)
+        tabs = kept("tabs", T, U8)
+        w2w = kept("w2w", 2 * H, U8)
+        w2s = kept("w2s", H, U8)
+        tab2w = [kept(f"tab2w{a}", TB, U32) for a in range(2)]
+        tab2s = kept("tab2s", TB, U8)
+        w5w = [kept(f"w5w{a}", N, U32) for a in range(2)]
+        w5s = kept("w5s", N, U8)
+        gain_sb = kept("gain_sb", 2 * PACK, F32)
+        low_sb = kept("low_sb", N // P, F32)
+
+        nc.gpsimd.memset(w2s[:].bitcast(I32), 0)
+        for plane in (tabs, tab2s, w5s):
+            nc.vector.memset(plane[:].bitcast(I32), 0)
+
+        nc.sync.dma_start(offs_sb[:], offs)
+        nc.sync.dma_start(offs2_sb[:], offs2)
+        nc.sync.dma_start(pos1_sb[:], pos1)
+        load_scales(nc.scalar, tabs, tab_scales)
+        load_scales(nc.gpsimd, w2s, w2_scales)
+        nc.sync.dma_start(out=w2w[:].bitcast(I32), in_=w2_words[0].bitcast(I32))
+        nc.sync.dma_start(out=tabw[:].bitcast(I32), in_=words_of(tab_words[0]))
+        raw = {"w1a": load_halves("w1a", w1, 0, 0), "w1b": load_halves("w1b", w1, 0, BANK)}
+        nc.sync.dma_start(
+            out=gain_sb[:].rearrange("p (a t) -> p a t", t=PACK),
+            in_=gain.rearrange("(a p t) -> p a t", p=P, t=PACK),
+        )
+        for a in range(2):
+            nc.sync.dma_start(out=tab2w[a][:].bitcast(I32), in_=words_of(tab2_words[a]))
+        raw["w3a"] = load_rows("w3a", w3, 0, 0)
+        raw["w3b"] = load_rows("w3b", w3, 1, 0)
+        load_scales(nc.sync, tab2s, tab2_scales)
+        load_scales(nc.sync, w5s, w5_scales)
+        raw["w4a"] = load_rows("w4a", w4, 0, 0)
+        raw["w4b"] = load_rows("w4b", w4, 1, 0)
+        for a in range(2):
+            nc.sync.dma_start(out=w5w[a][:].bitcast(I32), in_=words_of(w5_words[a]))
+        with nc.allow_non_contiguous_dma(reason="one offset a partition"):
+            nc.sync.dma_start(out=low_sb[:], in_=low.rearrange("(n p) -> p n", p=P))
+
+        def copy_on(engine, out_ap, in_ap):
+            if engine == "scalar":
+                nc.scalar.copy(out=out_ap, in_=in_ap)
+            elif engine == "gpsimd":
+                nc.gpsimd.tensor_scalar(out=out_ap, in0=in_ap, scalar1=1.0, scalar2=0.0, op0=ALU.mult, op1=ALU.add)
+            else:
+                nc.vector.tensor_copy(out=out_ap, in_=in_ap)
+
+        rounded = {name: kept(name + "g", PACK * BANK, BF16) for name in ("w1a", "w1b", "w3a", "w3b", "w4a", "w4b")}
+        codes = {name: kept(name + "c", BANK, U32) for name in list(rounded) + ["h00", "h01", "h10", "h11"]}
+        scales = {name: kept(name + "s", BANK, U8) for name in codes}
+
+        def quantise(name):
+            nc.vector.quantize_mx(out=codes[name][:].bitcast(FP8X4), scales=scales[name][:], in_=rounded[name][:])
+
+        def round_plain(name, u, engine):
+            dst = rounded[name][:].rearrange("p (c i j) -> p c j i", i=4, j=PACK)
+            copy_on(engine, dst[:, 64 * u : 64 * (u + 1)], raw[name][u].rearrange("p j (c i) -> p c j i", i=4))
+
+        def round_dealt(name, u, engine):
+            dst = rounded[name][:].rearrange("p (t m j) -> p m j t", t=PACK, j=PACK)
+            copy_on(engine, dst[:, 64 * u : 64 * (u + 1)], raw[name][u].rearrange("p j (m t) -> p m j t", t=PACK))
+
+        vw = [kept(f"vw{jh}", BANK, U32) for jh in range(2)]
+        vs = [kept(f"vs{jh}", BANK, U8) for jh in range(2)]
+        cuts = [offs_sb[:, jh * (BANK // 16) : (jh + 1) * (BANK // 16)] for jh in range(2)]
+        v2w = [kept(f"v2w{a}", PICK, U32) for a in range(2)]
+        v2s = kept("v2s", PICK, U8)
+        w2d = kept("w2d", 2 * H, U8)
+        w2ds = kept("w2ds", H, U8)
+        y = [kept(f"y{n}", S, F32) for n in range(N // P)]
+
+        def first_stage(jh, a, pair):
+            w1c, w1s = codes["w1" + "ab"[a]], scales["w1" + "ab"[a]]
+            least = ring.tile([P, PAIR, PACK], F32, name="least")
+            for u in range(2):
+                c0 = pair * PAIR + u * CHUNK
+                cols = slice(c0, c0 + CHUNK)
+                d1 = psum.tile([P, PACK, CHUNK], F32, name="d1", bufs=2)
+                d2 = psum.tile([P, PACK, CHUNK], F32, name="d2", bufs=3)
+                for t in range(PACK):
+                    rows = slice(t * P, (t + 1) * P)
+                    nc.tensor.matmul_mx(
+                        out=d1[:, t, :], lhsT=w1c[:, rows].bitcast(FP8X4), lhsT_scale=w1s[:, rows],
+                        rhs=vw[jh][:, cols].bitcast(FP8X4), rhs_scale=vs[jh][:, cols], start=True, stop=True,
+                    )
+                for t in range(PACK):
+                    r0 = a * PASS + t * P
+                    nc.tensor.matmul_mx(
+                        out=d2[:, t, :], lhsT=w2d[:, 2 * r0 : 2 * (r0 + P)].bitcast(FP4X4),
+                        lhsT_scale=w2ds[:, r0 : r0 + P],
+                        rhs=vw[jh][:, cols].bitcast(FP8X4), rhs_scale=vs[jh][:, cols], start=True, stop=True,
+                    )
+                d1_sb = ring.tile([P, CHUNK, PACK], F32, name="d1_sb")
+                nc.scalar.copy(out=d1_sb[:], in_=d1[:].rearrange("p t c -> p c t"))
+                nc.vector.tensor_tensor(
+                    out=least[:, u * CHUNK : (u + 1) * CHUNK, :], in0=d2[:].rearrange("p t c -> p c t"),
+                    in1=d1_sb[:], op=ALU.min,
+                )
+            bent = ring.tile([P, PAIR, PACK], F32, name="bent")
+            nc.scalar.activation(out=bent[:], in_=least[:], func=ACT.Tanh)
+            h16 = ring.tile([P, PAIR, PACK], BF16, name="h16", align_bytes=64)
+            gains = gain_sb[:, a * PACK : (a + 1) * PACK].unsqueeze(1).to_broadcast([P, PAIR, PACK])
+            nc.vector.tensor_tensor(out=h16[:], in0=bent[:], in1=gains, op=ALU.mult)
+            cols = slice(pair * PAIR, (pair + 1) * PAIR)
+            nc.vector.quantize_mx(
+                out=codes[f"h{jh}{a}"][:, cols].bitcast(FP8X4), scales=scales[f"h{jh}{a}"][:, cols],
+                in_=h16[:].rearrange("p c t -> p (c t)"),
+            )
+
+        def own(prefix, suffixes):
+            return [(codes[prefix + x], scales[prefix + x], 0) for x in suffixes]
+
+        def product(tag, bufs, lhs, rhs, n):
+            acc = psum.tile([P, BANK], F32, name=tag, bufs=bufs)
+            rows = slice(n * P, (n + 1) * P)
+            for a in range(2):
+                (lc, ls, lk), (rc, rs, rk) = lhs[a], rhs[a]
+                nc.tensor.matmul_mx(
+                    out=acc[:], lhsT=lc[:, rows].bitcast(FP8X4), lhsT_scale=ls[lk:P, rows],
+                    rhs=rc[:].bitcast(FP8X4), rhs_scale=rs[rk:P, :], start=(a == 0), stop=(a == 1),
+                )
+            return acc
+
+        def second_stage(jh, n):
+            acc = product("acc", 3, own("w3", "ab"), own(f"h{jh}", "01"), n)
+            nc.scalar.copy(out=y[n][:, jh * BANK : (jh + 1) * BANK], in_=acc[:])
+
+        def deal_words():
+            nc.vector.tensor_copy(
+                out=w2d[:].bitcast(U16).rearrange("p (a t m) -> p a t m", a=2, t=PACK),
+                in_=w2w[:].bitcast(U16).rearrange("p (a m t) -> p a t m", a=2, t=PACK),
+            )
+
+        def deal_scales():
+            nc.vector.tensor_copy(
+                out=w2ds[:].rearrange("p (a t m) -> p a t m", a=2, t=PACK),
+                in_=w2s[:].rearrange("p (a m t) -> p a t m", a=2, t=PACK),
+            )
+
+        deal_words()
+        for jh in range(2):
+            nc.vector.tensor_copy(vs[jh][:], tabs[:].indirect(cuts[jh]))
+        nc.vector.tensor_copy(vw[0][:], tabw[:].indirect(cuts[0]))
+        deal_scales()
+        round_dealt("w1a", 0, "scalar")
+        round_dealt("w1a", 1, "vector")
+        quantise("w1a")
+        nc.vector.tensor_copy(vw[1][:], tabw[:].indirect(cuts[1]))
+        round_dealt("w1b", 0, "scalar")
+
+        first_stage(0, 0, 0)
+        round_dealt("w1b", 1, "scalar")
+        quantise("w1b")
+        first_stage(0, 0, 1)
+        round_plain("w3a", 0, "scalar")
+        nc.vector.tensor_copy(v2w[0][:], tab2w[0][:].indirect(offs2_sb[:]))
+        first_stage(0, 1, 0)
+        round_plain("w3a", 1, "scalar")
+        quantise("w3a")
+        first_stage(0, 1, 1)
+        round_plain("w3b", 0, "scalar")
+        nc.vector.tensor_copy(v2w[1][:], tab2w[1][:].indirect(offs2_sb[:]))
+        first_stage(1, 0, 0)
+        round_plain("w3b", 1, "scalar")
+        quantise("w3b")
+        round_plain("w4a", 0, "vector")
+        first_stage(1, 0, 1)
+        second_stage(0, 0)
+        second_stage(0, 1)
+        nc.vector.tensor_copy(v2s[:], tab2s[:].indirect(offs2_sb[:]))
+        first_stage(1, 1, 0)
+        second_stage(0, 2)
+        second_stage(0, 3)
+        round_plain("w4a", 1, "vector")
+        quantise("w4a")
+        first_stage(1, 1, 1)
+        round_plain("w4b", 0, "scalar")
+        round_plain("w4b", 1, "scalar")
+        for n in range(N // P):
+            second_stage(1, n)
+        quantise("w4b")
+
+        v2 = [(v2w[a], v2s, 4 * a) for a in range(2)]
+        w5q = [(w5w[a], w5s, 4 * a) for a in range(2)]
+        picked = [kept(f"picked{n}", PICK, F32) for n in range(N // P)]
+
+        def pick(n):
+            nc.vector.tensor_copy(picked[n][:], y[n][:].indirect(pos1_sb[:]))
+
+        def finish(n):
+            cap = product("d2", 3, own("w4", "ab"), v2, n)
+            base = product("d1", 2, w5q, v2, n)
+            capped = ring.tile([P, PICK], F32, name="capped")
+            nc.vector.tensor_tensor(out=capped[:], in0=cap[:], in1=picked[n][:], op=ALU.min)
+            result = kept(f"result{n}", PICK, F32)
+            nc.vector.scalar_tensor_tensor(
+                out=result[:], in0=base[:], scalar=low_sb[:, n : n + 1], in1=capped[:], op0=ALU.add, op1=ALU.max,
+            )
+            nc.sync.dma_start(out=out[n * P : (n + 1) * P, :], in_=result[:])
+
+        for n in range(N // P):
+            pick(n)
+        for n in range(N // P):
+            finish(n)

@@ -73,22 +73,24 @@ def tile_list_crystal_deposit_grading_kernel(
         gain_sb = kept("gain_sb", 2 * PACK, F32)
         low_sb = kept("low_sb", N // P, F32)
 
-        nc.gpsimd.memset(w2s[:].bitcast(I32), 0)
-        for plane in (tabs, tab2s, w5s):
+        for plane in (tabs, w2s, tab2s, w5s):
             nc.vector.memset(plane[:].bitcast(I32), 0)
 
         nc.sync.dma_start(offs_sb[:], offs)
         nc.sync.dma_start(offs2_sb[:], offs2)
         nc.sync.dma_start(pos1_sb[:], pos1)
-        load_scales(nc.scalar, tabs, tab_scales)
-        load_scales(nc.gpsimd, w2s, w2_scales)
-        nc.sync.dma_start(out=w2w[:].bitcast(I32), in_=w2_words[0].bitcast(I32))
-        nc.sync.dma_start(out=tabw[:].bitcast(I32), in_=words_of(tab_words[0]))
-        raw = {"w1a": load_halves("w1a", w1, 0, 0), "w1b": load_halves("w1b", w1, 0, BANK)}
         nc.sync.dma_start(
             out=gain_sb[:].rearrange("p (a t) -> p a t", t=PACK),
             in_=gain.rearrange("(a p t) -> p a t", p=P, t=PACK),
         )
+        raw = {"w1a": load_halves("w1a", w1, 0, 0)}
+        nc.sync.dma_start(out=w2w[:].bitcast(I32), in_=w2_words[0].bitcast(I32))
+        with nc.allow_non_contiguous_dma(reason="one offset a partition"):
+            nc.sync.dma_start(out=low_sb[:], in_=low.rearrange("(n p) -> p n", p=P))
+        load_scales(nc.sync, tabs, tab_scales)
+        nc.sync.dma_start(out=tabw[:].bitcast(I32), in_=words_of(tab_words[0]))
+        load_scales(nc.sync, w2s, w2_scales)
+        raw["w1b"] = load_halves("w1b", w1, 0, BANK)
         for a in range(2):
             nc.sync.dma_start(out=tab2w[a][:].bitcast(I32), in_=words_of(tab2_words[a]))
         raw["w3a"] = load_rows("w3a", w3, 0, 0)
@@ -99,8 +101,6 @@ def tile_list_crystal_deposit_grading_kernel(
         raw["w4b"] = load_rows("w4b", w4, 1, 0)
         for a in range(2):
             nc.sync.dma_start(out=w5w[a][:].bitcast(I32), in_=words_of(w5_words[a]))
-        with nc.allow_non_contiguous_dma(reason="one offset a partition"):
-            nc.sync.dma_start(out=low_sb[:], in_=low.rearrange("(n p) -> p n", p=P))
 
         def copy_on(engine, out_ap, in_ap):
             if engine == "scalar":
@@ -134,43 +134,74 @@ def tile_list_crystal_deposit_grading_kernel(
         w2ds = kept("w2ds", H, U8)
         y = [kept(f"y{n}", S, F32) for n in range(N // P)]
 
-        def first_stage(jh, a, pair):
+        steps = [(jh, a, pair) for jh in range(2) for a in range(2) for pair in range(2)]
+        banks, least, bent, h16 = {}, {}, {}, {}
+
+        def readings(s, u):
+            jh, a, pair = steps[s]
             w1c, w1s = codes["w1" + "ab"[a]], scales["w1" + "ab"[a]]
-            least = ring.tile([P, PAIR, PACK], F32, name="least")
-            for u in range(2):
-                c0 = pair * PAIR + u * CHUNK
-                cols = slice(c0, c0 + CHUNK)
-                d1 = psum.tile([P, PACK, CHUNK], F32, name="d1", bufs=2)
-                d2 = psum.tile([P, PACK, CHUNK], F32, name="d2", bufs=3)
-                for t in range(PACK):
-                    rows = slice(t * P, (t + 1) * P)
-                    nc.tensor.matmul_mx(
-                        out=d1[:, t, :], lhsT=w1c[:, rows].bitcast(FP8X4), lhsT_scale=w1s[:, rows],
-                        rhs=vw[jh][:, cols].bitcast(FP8X4), rhs_scale=vs[jh][:, cols], start=True, stop=True,
-                    )
-                for t in range(PACK):
-                    r0 = a * PASS + t * P
-                    nc.tensor.matmul_mx(
-                        out=d2[:, t, :], lhsT=w2d[:, 2 * r0 : 2 * (r0 + P)].bitcast(FP4X4),
-                        lhsT_scale=w2ds[:, r0 : r0 + P],
-                        rhs=vw[jh][:, cols].bitcast(FP8X4), rhs_scale=vs[jh][:, cols], start=True, stop=True,
-                    )
-                d1_sb = ring.tile([P, CHUNK, PACK], F32, name="d1_sb")
-                nc.scalar.copy(out=d1_sb[:], in_=d1[:].rearrange("p t c -> p c t"))
-                nc.vector.tensor_tensor(
-                    out=least[:, u * CHUNK : (u + 1) * CHUNK, :], in0=d2[:].rearrange("p t c -> p c t"),
-                    in1=d1_sb[:], op=ALU.min,
+            c0 = pair * PAIR + u * CHUNK
+            cols = slice(c0, c0 + CHUNK)
+            d1 = psum.tile([P, PACK, CHUNK], F32, name="d1", bufs=2)
+            d2 = psum.tile([P, PACK, CHUNK], F32, name="d2", bufs=3)
+            for t in range(PACK):
+                rows = slice(t * P, (t + 1) * P)
+                nc.tensor.matmul_mx(
+                    out=d1[:, t, :], lhsT=w1c[:, rows].bitcast(FP8X4), lhsT_scale=w1s[:, rows],
+                    rhs=vw[jh][:, cols].bitcast(FP8X4), rhs_scale=vs[jh][:, cols], start=True, stop=True,
                 )
-            bent = ring.tile([P, PAIR, PACK], F32, name="bent")
-            nc.scalar.activation(out=bent[:], in_=least[:], func=ACT.Tanh)
-            h16 = ring.tile([P, PAIR, PACK], BF16, name="h16", align_bytes=64)
-            gains = gain_sb[:, a * PACK : (a + 1) * PACK].unsqueeze(1).to_broadcast([P, PAIR, PACK])
-            nc.vector.tensor_tensor(out=h16[:], in0=bent[:], in1=gains, op=ALU.mult)
-            cols = slice(pair * PAIR, (pair + 1) * PAIR)
+            for t in range(PACK):
+                r0 = a * PASS + t * P
+                nc.tensor.matmul_mx(
+                    out=d2[:, t, :], lhsT=w2d[:, 2 * r0 : 2 * (r0 + P)].bitcast(FP4X4),
+                    lhsT_scale=w2ds[:, r0 : r0 + P],
+                    rhs=vw[jh][:, cols].bitcast(FP8X4), rhs_scale=vs[jh][:, cols], start=True, stop=True,
+                )
+            d1_sb = ring.tile([P, CHUNK, PACK], F32, name="d1_sb")
+            nc.scalar.copy(out=d1_sb[:], in_=d1[:].rearrange("p t c -> p c t"))
+            banks[s, u] = (d1_sb, d2)
+
+        def take_least(s, u):
+            if u == 0:
+                least[s] = ring.tile([P, PAIR, PACK], F32, name="least")
+            d1_sb, d2 = banks[s, u]
+            nc.vector.tensor_tensor(
+                out=least[s][:, u * CHUNK : (u + 1) * CHUNK, :], in0=d2[:].rearrange("p t c -> p c t"),
+                in1=d1_sb[:], op=ALU.min,
+            )
+
+        def bend(s, lo=0, hi=PAIR):
+            if lo == 0:
+                bent[s] = ring.tile([P, PAIR, PACK], F32, name="bent")
+            nc.scalar.activation(out=bent[s][:, lo:hi, :], in_=least[s][:, lo:hi, :], func=ACT.Tanh)
+
+        def apply_gain(s, lo=0, hi=PAIR, engine="vector"):
+            a = steps[s][1]
+            if lo == 0:
+                h16[s] = ring.tile([P, PAIR, PACK], BF16, name="h16", align_bytes=64)
+            gains = gain_sb[:, a * PACK : (a + 1) * PACK].unsqueeze(1).to_broadcast([P, hi - lo, PACK])
+            unit = nc.vector if engine == "vector" else nc.gpsimd
+            unit.tensor_tensor(out=h16[s][:, lo:hi, :], in0=bent[s][:, lo:hi, :], in1=gains, op=ALU.mult)
+
+        def quantise_h(s, lo=0, hi=PAIR):
+            jh, a, pair = steps[s]
+            cols = slice(pair * PAIR + lo, pair * PAIR + hi)
             nc.vector.quantize_mx(
                 out=codes[f"h{jh}{a}"][:, cols].bitcast(FP8X4), scales=scales[f"h{jh}{a}"][:, cols],
-                in_=h16[:].rearrange("p c t -> p (c t)"),
+                in_=h16[s][:, lo:hi, :].rearrange("p c t -> p (c t)"),
             )
+
+        def first_stage(s):
+            readings(s, 0)
+            readings(s, 1)
+            if s >= 2:
+                apply_gain(s - 2)
+            take_least(s, 0)
+            if s >= 2:
+                quantise_h(s - 2)
+            take_least(s, 1)
+            if s >= 1:
+                bend(s - 1)
 
         def own(prefix, suffixes):
             return [(codes[prefix + x], scales[prefix + x], 0) for x in suffixes]
@@ -196,53 +227,62 @@ def tile_list_crystal_deposit_grading_kernel(
                 in_=w2w[:].bitcast(U16).rearrange("p (a m t) -> p a t m", a=2, t=PACK),
             )
 
-        def deal_scales():
+        def deal_scales(a):
+            cols = slice(a * PASS, (a + 1) * PASS)
             nc.vector.tensor_copy(
-                out=w2ds[:].rearrange("p (a t m) -> p a t m", a=2, t=PACK),
-                in_=w2s[:].rearrange("p (a m t) -> p a t m", a=2, t=PACK),
+                out=w2ds[:, cols].rearrange("p (t m) -> p t m", t=PACK),
+                in_=w2s[:, cols].rearrange("p (m t) -> p t m", t=PACK),
             )
 
+        round_dealt("w1a", 0, "scalar")
+        round_dealt("w1a", 1, "vector")
+        quantise("w1a")
         deal_words()
         for jh in range(2):
             nc.vector.tensor_copy(vs[jh][:], tabs[:].indirect(cuts[jh]))
         nc.vector.tensor_copy(vw[0][:], tabw[:].indirect(cuts[0]))
-        deal_scales()
-        round_dealt("w1a", 0, "scalar")
-        round_dealt("w1a", 1, "vector")
-        quantise("w1a")
+        deal_scales(0)
         nc.vector.tensor_copy(vw[1][:], tabw[:].indirect(cuts[1]))
         round_dealt("w1b", 0, "scalar")
 
-        first_stage(0, 0, 0)
+        first_stage(0)
+        deal_scales(1)
         round_dealt("w1b", 1, "scalar")
         quantise("w1b")
-        first_stage(0, 0, 1)
+        first_stage(1)
         round_plain("w3a", 0, "scalar")
         nc.vector.tensor_copy(v2w[0][:], tab2w[0][:].indirect(offs2_sb[:]))
-        first_stage(0, 1, 0)
+        first_stage(2)
         round_plain("w3a", 1, "scalar")
         quantise("w3a")
-        first_stage(0, 1, 1)
+        first_stage(3)
         round_plain("w3b", 0, "scalar")
         nc.vector.tensor_copy(v2w[1][:], tab2w[1][:].indirect(offs2_sb[:]))
-        first_stage(1, 0, 0)
+        first_stage(4)
         round_plain("w3b", 1, "scalar")
         quantise("w3b")
         round_plain("w4a", 0, "vector")
-        first_stage(1, 0, 1)
+        first_stage(5)
+        round_plain("w4b", 0, "scalar")
+        nc.vector.tensor_copy(v2s[:], tab2s[:].indirect(offs2_sb[:]))
+        first_stage(6)
         second_stage(0, 0)
         second_stage(0, 1)
-        nc.vector.tensor_copy(v2s[:], tab2s[:].indirect(offs2_sb[:]))
-        first_stage(1, 1, 0)
+        round_plain("w4a", 1, "vector")
+        first_stage(7)
+        bend(7, 0, CHUNK)
+        apply_gain(6)
+        bend(7, CHUNK, PAIR)
+        quantise_h(6)
+        apply_gain(7, 0, CHUNK)
+        apply_gain(7, CHUNK, PAIR)
+        quantise_h(7)
         second_stage(0, 2)
         second_stage(0, 3)
-        round_plain("w4a", 1, "vector")
-        quantise("w4a")
-        first_stage(1, 1, 1)
-        round_plain("w4b", 0, "scalar")
         round_plain("w4b", 1, "scalar")
         for n in range(N // P):
             second_stage(1, n)
+        quantise("w4a")
         quantise("w4b")
 
         v2 = [(v2w[a], v2s, 4 * a) for a in range(2)]

@@ -1,6 +1,7 @@
 from contextlib import ExitStack
 
 import concourse.mybir as mybir
+from concourse.masks import make_identity
 
 K, H, N, T, S, M, TB, PICK = 512, 1024, 512, 4096, 1024, 1024, 2048, 512
 FLOPS = 2 * (2 * K * H * S + H * N * S + 2 * M * N * PICK)
@@ -22,6 +23,8 @@ PASS = P * PACK
 BANK = 512
 CHUNK = BANK // PACK
 PAIR = 2 * CHUNK
+POOL_STEPS = 0
+POOL_CUT = 64
 
 
 def tile_list_crystal_deposit_grading_kernel(
@@ -47,7 +50,7 @@ def tile_list_crystal_deposit_grading_kernel(
                 queue.dma_start(out=plane[32 * q : 32 * q + 4 * passes, :].bitcast(I32), in_=rows.bitcast(I32))
 
         def load_block(name, w, a, c0, width):
-            raw = keep.tile([P, PACK, width], F32, name=name)
+            raw = keep.tile([P, PACK, width], F32, name=name, tag=name)
             rows = w[a * PASS : (a + 1) * PASS, c0 : c0 + width]
             nc.sync.dma_start(out=raw[:], in_=rows.rearrange("(p j) c -> p j c", j=PACK))
             return raw
@@ -76,29 +79,29 @@ def tile_list_crystal_deposit_grading_kernel(
         for plane in (tabs, w2s, tab2s, w5s):
             nc.vector.memset(plane[:].bitcast(I32), 0)
 
+        raw = {"w1a": []}
         nc.sync.dma_start(offs_sb[:], offs)
         nc.sync.dma_start(offs2_sb[:], offs2)
         nc.sync.dma_start(pos1_sb[:], pos1)
         nc.sync.dma_start(
-            out=gain_sb[:].rearrange("p (a t) -> p a t", t=PACK),
+            out=gain_sb[:, 0 : 2 * PACK].rearrange("p (a t) -> p a t", t=PACK),
             in_=gain.rearrange("(a p t) -> p a t", p=P, t=PACK),
         )
-        raw = {"w1a": load_halves("w1a", w1, 0, 0)}
-        nc.sync.dma_start(out=w2w[:].bitcast(I32), in_=w2_words[0].bitcast(I32))
         with nc.allow_non_contiguous_dma(reason="one offset a partition"):
             nc.sync.dma_start(out=low_sb[:], in_=low.rearrange("(n p) -> p n", p=P))
+        raw["w1a"].append(load_block("w1a_0", w1, 0, 0, PAIR)[:])
+        raw["w1a"].append(load_block("w1a_1", w1, 0, PAIR, PAIR)[:])
+        nc.sync.dma_start(out=w2w[:].bitcast(I32), in_=w2_words[0].bitcast(I32))
         load_scales(nc.sync, tabs, tab_scales)
         nc.sync.dma_start(out=tabw[:].bitcast(I32), in_=words_of(tab_words[0]))
         load_scales(nc.sync, w2s, w2_scales)
         raw["w1b"] = load_halves("w1b", w1, 0, BANK)
         for a in range(2):
             nc.sync.dma_start(out=tab2w[a][:].bitcast(I32), in_=words_of(tab2_words[a]))
-        raw["w3a"] = load_rows("w3a", w3, 0, 0)
-        raw["w3b"] = load_rows("w3b", w3, 1, 0)
+        raw["w3"] = [load_block(f"w3raw{a}", w3, a, 0, BANK) for a in range(2)]
         load_scales(nc.sync, tab2s, tab2_scales)
         load_scales(nc.sync, w5s, w5_scales)
-        raw["w4a"] = load_rows("w4a", w4, 0, 0)
-        raw["w4b"] = load_rows("w4b", w4, 1, 0)
+        raw["w4"] = [load_block(f"w4raw{a}", w4, a, 0, BANK) for a in range(2)]
         for a in range(2):
             nc.sync.dma_start(out=w5w[a][:].bitcast(I32), in_=words_of(w5_words[a]))
 
@@ -110,16 +113,26 @@ def tile_list_crystal_deposit_grading_kernel(
             else:
                 nc.vector.tensor_copy(out=out_ap, in_=in_ap)
 
-        rounded = {name: kept(name + "g", PACK * BANK, BF16) for name in ("w1a", "w1b", "w3a", "w3b", "w4a", "w4b")}
-        codes = {name: kept(name + "c", BANK, U32) for name in list(rounded) + ["h00", "h01", "h10", "h11"]}
-        scales = {name: kept(name + "s", BANK, U8) for name in codes}
+        widths = {"w1a": BANK, "w1b": BANK, "w3": 2 * BANK, "w4": 2 * BANK, "h0": 2 * BANK, "h1": 2 * BANK}
+        rounded = {name: kept(name + "g", PACK * width, BF16) for name, width in widths.items()}
+        codes = {name: kept(name + "c", width, U32) for name, width in widths.items()}
+        scales = {name: kept(name + "s", width, U8) for name, width in widths.items()}
 
-        def quantise(name):
-            nc.vector.quantize_mx(out=codes[name][:].bitcast(FP8X4), scales=scales[name][:], in_=rounded[name][:])
+        def quantise(name, lo, hi):
+            nc.vector.quantize_mx(
+                out=codes[name][:, lo:hi].bitcast(FP8X4), scales=scales[name][:, lo:hi],
+                in_=rounded[name][:, PACK * lo : PACK * hi],
+            )
 
-        def round_plain(name, u, engine):
-            dst = rounded[name][:].rearrange("p (c i j) -> p c j i", i=4, j=PACK)
-            copy_on(engine, dst[:, 64 * u : 64 * (u + 1)], raw[name][u].rearrange("p j (c i) -> p c j i", i=4))
+        def round_plain(name, a, lo, hi, engine):
+            dst = rounded[name][:, PACK * (a * BANK + lo) : PACK * (a * BANK + hi)]
+            if engine == "gpsimd":
+                copy_on(engine, dst.rearrange("p (c j) -> p c j", j=PACK), raw[name][a][:, :, lo:hi].rearrange("p j c -> p c j"))
+                return
+            copy_on(
+                engine, dst.rearrange("p (c i j) -> p c j i", i=4, j=PACK),
+                raw[name][a][:, :, lo:hi].rearrange("p j (c i) -> p c j i", i=4),
+            )
 
         def round_dealt(name, u, engine):
             dst = rounded[name][:].rearrange("p (t m j) -> p m j t", t=PACK, j=PACK)
@@ -135,7 +148,7 @@ def tile_list_crystal_deposit_grading_kernel(
         y = [kept(f"y{n}", S, F32) for n in range(N // P)]
 
         steps = [(jh, a, pair) for jh in range(2) for a in range(2) for pair in range(2)]
-        banks, least, bent, h16 = {}, {}, {}, {}
+        banks, least, bent = {}, {}, {}
 
         def readings(s, u):
             jh, a, pair = steps[s]
@@ -157,54 +170,49 @@ def tile_list_crystal_deposit_grading_kernel(
                     lhsT_scale=w2ds[:, r0 : r0 + P],
                     rhs=vw[jh][:, cols].bitcast(FP8X4), rhs_scale=vs[jh][:, cols], start=True, stop=True,
                 )
-            d1_sb = ring.tile([P, CHUNK, PACK], F32, name="d1_sb")
-            nc.scalar.copy(out=d1_sb[:], in_=d1[:].rearrange("p t c -> p c t"))
+            d1_sb = ring.tile([P, CHUNK // 2, PACK, 2], F32, name="d1_sb")
+            nc.scalar.copy(out=d1_sb[:], in_=d1[:].rearrange("p t (c i) -> p c t i", i=2))
             banks[s, u] = (d1_sb, d2)
 
         def take_least(s, u):
             if u == 0:
-                least[s] = ring.tile([P, PAIR, PACK], F32, name="least")
+                least[s] = ring.tile([P, PAIR // 2, PACK, 2], F32, name="least")
             d1_sb, d2 = banks[s, u]
             nc.vector.tensor_tensor(
-                out=least[s][:, u * CHUNK : (u + 1) * CHUNK, :], in0=d2[:].rearrange("p t c -> p c t"),
+                out=least[s][:, u * CHUNK // 2 : (u + 1) * CHUNK // 2], in0=d2[:].rearrange("p t (c i) -> p c t i", i=2),
                 in1=d1_sb[:], op=ALU.min,
             )
 
         def bend(s, lo=0, hi=PAIR):
             if lo == 0:
-                bent[s] = ring.tile([P, PAIR, PACK], F32, name="bent")
-            nc.scalar.activation(out=bent[s][:, lo:hi, :], in_=least[s][:, lo:hi, :], func=ACT.Tanh)
-
-        def apply_gain(s, lo=0, hi=PAIR, engine="vector"):
-            a = steps[s][1]
-            if lo == 0:
-                h16[s] = ring.tile([P, PAIR, PACK], BF16, name="h16", align_bytes=64)
-            gains = gain_sb[:, a * PACK : (a + 1) * PACK].unsqueeze(1).to_broadcast([P, hi - lo, PACK])
-            unit = nc.vector if engine == "vector" else nc.gpsimd
-            unit.tensor_tensor(out=h16[s][:, lo:hi, :], in0=bent[s][:, lo:hi, :], in1=gains, op=ALU.mult)
-
-        def quantise_h(s, lo=0, hi=PAIR):
-            jh, a, pair = steps[s]
-            cols = slice(pair * PAIR + lo, pair * PAIR + hi)
-            nc.vector.quantize_mx(
-                out=codes[f"h{jh}{a}"][:, cols].bitcast(FP8X4), scales=scales[f"h{jh}{a}"][:, cols],
-                in_=h16[s][:, lo:hi, :].rearrange("p c t -> p (c t)"),
+                bent[s] = ring.tile([P, PAIR, PACK], F32, name="bent", bufs=3)
+            nc.scalar.activation(
+                out=bent[s][:, lo:hi, :].rearrange("p (c i) t -> p c i t", i=2),
+                in_=least[s][:, lo // 2 : hi // 2].rearrange("p c t i -> p c i t"), func=ACT.Tanh,
             )
+
+        def apply_gain(s, lo, hi, unit, gains):
+            jh, a, pair = steps[s]
+            c0 = a * BANK + pair * PAIR
+            dst = rounded[f"h{jh}"][:, PACK * (c0 + lo) : PACK * (c0 + hi)].rearrange("p (c t) -> p c t", t=PACK)
+            spread = gains[:, a * PACK : (a + 1) * PACK].unsqueeze(1).to_broadcast([P, hi - lo, PACK])
+            unit.tensor_tensor(out=dst, in0=bent[s][:, lo:hi, :], in1=spread, op=ALU.mult)
 
         def first_stage(s):
             readings(s, 0)
             readings(s, 1)
-            if s >= 2:
-                apply_gain(s - 2)
+            if s - 2 >= POOL_STEPS:
+                apply_gain(s - 2, 0, PAIR, nc.vector, gain_v)
             take_least(s, 0)
-            if s >= 2:
-                quantise_h(s - 2)
             take_least(s, 1)
             if s >= 1:
                 bend(s - 1)
+            if 0 <= s - 1 < POOL_STEPS:
+                for lo in range(0, PAIR, POOL_CUT):
+                    apply_gain(s - 1, lo, lo + POOL_CUT, nc.gpsimd, gain_sb)
 
-        def own(prefix, suffixes):
-            return [(codes[prefix + x], scales[prefix + x], 0) for x in suffixes]
+        def own(name):
+            return [(codes[name][:, a * BANK : (a + 1) * BANK], scales[name][:, a * BANK : (a + 1) * BANK], 0) for a in range(2)]
 
         def product(tag, bufs, lhs, rhs, n):
             acc = psum.tile([P, BANK], F32, name=tag, bufs=bufs)
@@ -213,12 +221,12 @@ def tile_list_crystal_deposit_grading_kernel(
                 (lc, ls, lk), (rc, rs, rk) = lhs[a], rhs[a]
                 nc.tensor.matmul_mx(
                     out=acc[:], lhsT=lc[:, rows].bitcast(FP8X4), lhsT_scale=ls[lk:P, rows],
-                    rhs=rc[:].bitcast(FP8X4), rhs_scale=rs[rk:P, :], start=(a == 0), stop=(a == 1),
+                    rhs=rc.bitcast(FP8X4), rhs_scale=rs[rk:P, :], start=(a == 0), stop=(a == 1),
                 )
             return acc
 
         def second_stage(jh, n):
-            acc = product("acc", 3, own("w3", "ab"), own(f"h{jh}", "01"), n)
+            acc = product("acc", 3, own("w3"), own(f"h{jh}"), n)
             nc.scalar.copy(out=y[n][:, jh * BANK : (jh + 1) * BANK], in_=acc[:])
 
         def deal_words():
@@ -234,58 +242,61 @@ def tile_list_crystal_deposit_grading_kernel(
                 in_=w2s[:, cols].rearrange("p (m t) -> p t m", t=PACK),
             )
 
+        gain_v = gain_sb
         round_dealt("w1a", 0, "scalar")
         round_dealt("w1a", 1, "vector")
-        quantise("w1a")
+        quantise("w1a", 0, BANK)
         deal_words()
         for jh in range(2):
             nc.vector.tensor_copy(vs[jh][:], tabs[:].indirect(cuts[jh]))
         nc.vector.tensor_copy(vw[0][:], tabw[:].indirect(cuts[0]))
         deal_scales(0)
         nc.vector.tensor_copy(vw[1][:], tabw[:].indirect(cuts[1]))
-        round_dealt("w1b", 0, "scalar")
 
         first_stage(0)
+        round_dealt("w1b", 0, "scalar")
         deal_scales(1)
-        round_dealt("w1b", 1, "scalar")
-        quantise("w1b")
+        round_dealt("w1b", 1, "vector")
+        quantise("w1b", 0, BANK)
         first_stage(1)
-        round_plain("w3a", 0, "scalar")
         nc.vector.tensor_copy(v2w[0][:], tab2w[0][:].indirect(offs2_sb[:]))
         first_stage(2)
-        round_plain("w3a", 1, "scalar")
-        quantise("w3a")
-        first_stage(3)
-        round_plain("w3b", 0, "scalar")
+        round_plain("w3", 0, 0 * PAIR, 1 * PAIR, "scalar")
         nc.vector.tensor_copy(v2w[1][:], tab2w[1][:].indirect(offs2_sb[:]))
+        first_stage(3)
+        round_plain("w3", 0, 1 * PAIR, 2 * PAIR, "scalar")
+        quantise("h0", 0, BANK)
         first_stage(4)
-        round_plain("w3b", 1, "scalar")
-        quantise("w3b")
-        round_plain("w4a", 0, "vector")
-        first_stage(5)
-        round_plain("w4b", 0, "scalar")
+        round_plain("w3", 1, 0 * PAIR, 1 * PAIR, "scalar")
         nc.vector.tensor_copy(v2s[:], tab2s[:].indirect(offs2_sb[:]))
+        first_stage(5)
+        round_plain("w3", 1, 1 * PAIR, 2 * PAIR, "scalar")
+        quantise("w3", 0, 2 * BANK)
+        quantise("h0", BANK, 2 * BANK)
         first_stage(6)
+        round_plain("w4", 0, 0 * PAIR, 1 * PAIR, "scalar")
         second_stage(0, 0)
-        second_stage(0, 1)
-        round_plain("w4a", 1, "vector")
         first_stage(7)
+        quantise("h1", 0, BANK)
+        second_stage(0, 1)
         bend(7, 0, CHUNK)
-        apply_gain(6)
+        apply_gain(6, 0, PAIR, nc.vector, gain_v)
         bend(7, CHUNK, PAIR)
-        quantise_h(6)
-        apply_gain(7, 0, CHUNK)
-        apply_gain(7, CHUNK, PAIR)
-        quantise_h(7)
+        apply_gain(7, 0, CHUNK, nc.vector, gain_v)
+        quantise("h1", BANK, BANK + PAIR)
+        apply_gain(7, CHUNK, PAIR, nc.vector, gain_v)
+        quantise("h1", BANK + PAIR, 2 * BANK)
         second_stage(0, 2)
         second_stage(0, 3)
-        round_plain("w4b", 1, "scalar")
+        round_plain("w4", 0, 1 * PAIR, 2 * PAIR, "scalar")
         for n in range(N // P):
             second_stage(1, n)
-        quantise("w4a")
-        quantise("w4b")
+        round_plain("w4", 1, 0 * PAIR, 1 * PAIR, "scalar")
+        round_plain("w4", 1, 1 * PAIR, 2 * PAIR, "scalar")
+        quantise("w4", 0, BANK)
+        quantise("w4", BANK, 2 * BANK)
 
-        v2 = [(v2w[a], v2s, 4 * a) for a in range(2)]
+        v2 = [(v2w[a][:], v2s, 4 * a) for a in range(2)]
         w5q = [(w5w[a], w5s, 4 * a) for a in range(2)]
         picked = [kept(f"picked{n}", PICK, F32) for n in range(N // P)]
 
@@ -293,11 +304,11 @@ def tile_list_crystal_deposit_grading_kernel(
             nc.vector.tensor_copy(picked[n][:], y[n][:].indirect(pos1_sb[:]))
 
         def finish(n):
-            cap = product("d2", 3, own("w4", "ab"), v2, n)
+            cap = product("d2", 3, own("w4"), v2, n)
             base = product("d1", 2, w5q, v2, n)
             capped = ring.tile([P, PICK], F32, name="capped")
             nc.vector.tensor_tensor(out=capped[:], in0=cap[:], in1=picked[n][:], op=ALU.min)
-            result = kept(f"result{n}", PICK, F32)
+            result = keep.tile([P, PICK], F32, name=f"result{n}", tag=f"w1{'ab'[n // 2]}_{n % 2}")
             nc.vector.scalar_tensor_tensor(
                 out=result[:], in0=base[:], scalar=low_sb[:, n : n + 1], in1=capped[:], op0=ALU.add, op1=ALU.max,
             )

@@ -170,26 +170,23 @@ def tile_list_crystal_deposit_grading_kernel(
                     lhsT_scale=w2ds[:, r0 : r0 + P],
                     rhs=vw[jh][:, cols].bitcast(FP8X4), rhs_scale=vs[jh][:, cols], start=True, stop=True,
                 )
-            d1_sb = ring.tile([P, CHUNK // 2, PACK, 2], F32, name="d1_sb")
-            nc.scalar.copy(out=d1_sb[:], in_=d1[:].rearrange("p t (c i) -> p c t i", i=2))
+            d1_sb = ring.tile([P, CHUNK, PACK], F32, name="d1_sb")
+            nc.scalar.copy(out=d1_sb[:], in_=d1[:].rearrange("p t c -> p c t"))
             banks[s, u] = (d1_sb, d2)
 
         def take_least(s, u):
             if u == 0:
-                least[s] = ring.tile([P, PAIR // 2, PACK, 2], F32, name="least")
+                least[s] = ring.tile([P, PAIR, PACK], F32, name="least")
             d1_sb, d2 = banks[s, u]
             nc.vector.tensor_tensor(
-                out=least[s][:, u * CHUNK // 2 : (u + 1) * CHUNK // 2], in0=d2[:].rearrange("p t (c i) -> p c t i", i=2),
+                out=least[s][:, u * CHUNK : (u + 1) * CHUNK, :], in0=d2[:].rearrange("p t c -> p c t"),
                 in1=d1_sb[:], op=ALU.min,
             )
 
         def bend(s, lo=0, hi=PAIR):
             if lo == 0:
                 bent[s] = ring.tile([P, PAIR, PACK], F32, name="bent", bufs=3)
-            nc.scalar.activation(
-                out=bent[s][:, lo:hi, :].rearrange("p (c i) t -> p c i t", i=2),
-                in_=least[s][:, lo // 2 : hi // 2].rearrange("p c t i -> p c i t"), func=ACT.Tanh,
-            )
+            nc.scalar.activation(out=bent[s][:, lo:hi, :], in_=least[s][:, lo:hi, :], func=ACT.Tanh)
 
         def apply_gain(s, lo, hi, unit, gains):
             jh, a, pair = steps[s]
@@ -274,7 +271,7 @@ def tile_list_crystal_deposit_grading_kernel(
         quantise("w3", 0, 2 * BANK)
         quantise("h0", BANK, 2 * BANK)
         first_stage(6)
-        round_plain("w4", 0, 0 * PAIR, 1 * PAIR, "scalar")
+        round_plain("w4", 0, 0 * PAIR, 1 * PAIR, "vector")
         second_stage(0, 0)
         first_stage(7)
         quantise("h1", 0, BANK)
@@ -288,10 +285,10 @@ def tile_list_crystal_deposit_grading_kernel(
         quantise("h1", BANK + PAIR, 2 * BANK)
         second_stage(0, 2)
         second_stage(0, 3)
-        round_plain("w4", 0, 1 * PAIR, 2 * PAIR, "scalar")
+        round_plain("w4", 0, 1 * PAIR, 2 * PAIR, "vector")
         for n in range(N // P):
             second_stage(1, n)
-        round_plain("w4", 1, 0 * PAIR, 1 * PAIR, "scalar")
+        round_plain("w4", 1, 0 * PAIR, 1 * PAIR, "vector")
         round_plain("w4", 1, 1 * PAIR, 2 * PAIR, "scalar")
         quantise("w4", 0, BANK)
         quantise("w4", BANK, 2 * BANK)

@@ -1,7 +1,6 @@
 from contextlib import ExitStack
 
 import concourse.mybir as mybir
-from concourse.masks import make_identity
 
 K, H, N, T, S, M, TB, PICK = 512, 1024, 512, 4096, 1024, 1024, 2048, 512
 FLOPS = 2 * (2 * K * H * S + H * N * S + 2 * M * N * PICK)
@@ -20,11 +19,17 @@ ACT = mybir.ActivationFunctionType
 P = 128
 PACK = 4
 PASS = P * PACK
+PASSES = 2
 BANK = 512
+BANKS = 8
+HALVES = S // BANK
 CHUNK = BANK // PACK
 PAIR = 2 * CHUNK
-POOL_STEPS = 0
-POOL_CUT = 64
+PIECE = BANK // 2
+LIST_ROWS = 16
+LINE = 4
+RING = 3
+TILES = N // P
 
 
 def tile_list_crystal_deposit_grading_kernel(
@@ -34,284 +39,275 @@ def tile_list_crystal_deposit_grading_kernel(
     nc = tc.nc
     with ExitStack() as ctx:
         keep = ctx.enter_context(tc.tile_pool(name="keep", bufs=1))
-        ring = ctx.enter_context(tc.tile_pool(name="ring", bufs=3))
-        psum = ctx.enter_context(tc.psum_pool(name="psum", bufs=1))
+        ring = ctx.enter_context(tc.tile_pool(name="ring", bufs=RING))
+        psum = ctx.enter_context(tc.psum_pool(name="psum", bufs=BANKS))
 
         def kept(name, width, dtype):
             return keep.tile([P, width], dtype, name=name, align_bytes=64)
 
-        def words_of(dram):
-            return dram.rearrange("p n t -> p (n t)").bitcast(I32)
+        def load_words(tile, dram):
+            nc.sync.dma_start(out=tile[:].bitcast(I32), in_=dram.rearrange("p n t -> p (n t)").bitcast(I32))
 
-        def load_scales(queue, plane, dram):
+        def load_plane(plane, dram):
             passes = dram.shape[0]
             for q in range(4):
                 rows = dram[:, 4 * q : 4 * q + 4, :] if passes > 1 else dram[0, 4 * q : 4 * q + 4, :]
-                queue.dma_start(out=plane[32 * q : 32 * q + 4 * passes, :].bitcast(I32), in_=rows.bitcast(I32))
+                nc.sync.dma_start(out=plane[32 * q : 32 * q + 4 * passes, :].bitcast(I32), in_=rows.bitcast(I32))
 
-        def load_block(name, w, a, c0, width):
-            raw = keep.tile([P, PACK, width], F32, name=name, tag=name)
-            rows = w[a * PASS : (a + 1) * PASS, c0 : c0 + width]
-            nc.sync.dma_start(out=raw[:], in_=rows.rearrange("(p j) c -> p j c", j=PACK))
-            return raw
+        def load_rows(name, w, a, first, width):
+            staged = keep.tile([P, PACK, width], F32, name=name, tag=name)
+            rows = w[a * PASS : (a + 1) * PASS, first : first + width]
+            nc.sync.dma_start(out=staged[:], in_=rows.rearrange("(p t) c -> p t c", t=PACK))
+            return staged
 
-        def load_rows(name, w, a, c0):
-            raw = load_block(name, w, a, c0, BANK)
-            return [raw[:, :, 0:PAIR], raw[:, :, PAIR:BANK]]
+        offs_sb = keep.tile([P, S // LIST_ROWS], U16, name="offs_sb")
+        offs2_sb = keep.tile([P, PICK // LIST_ROWS], U16, name="offs2_sb")
+        pos1_sb = keep.tile([P, PICK // LIST_ROWS], U16, name="pos1_sb")
+        tab_w = kept("tab_w", T, U32)
+        tab_s = kept("tab_s", T, U8)
+        w2_w = kept("w2_w", 2 * H, U8)
+        w2_s = kept("w2_s", H, U8)
+        tab2_w = [kept(f"tab2_w{a}", TB, U32) for a in range(PASSES)]
+        tab2_s = kept("tab2_s", TB, U8)
+        w5_w = [kept(f"w5_w{a}", N, U32) for a in range(PASSES)]
+        w5_s = kept("w5_s", N, U8)
+        gain_sb = kept("gain_sb", PASSES * PACK, F32)
+        low_sb = kept("low_sb", TILES, F32)
 
-        def load_halves(name, w, a, c0):
-            return [load_block(f"{name}_{u}", w, a, c0 + u * PAIR, PAIR)[:] for u in range(2)]
-
-        offs_sb = keep.tile([P, S // 16], U16, name="offs_sb")
-        offs2_sb = keep.tile([P, PICK // 16], U16, name="offs2_sb")
-        pos1_sb = keep.tile([P, PICK // 16], U16, name="pos1_sb")
-        tabw = kept("tabw", T, U32)
-        tabs = kept("tabs", T, U8)
-        w2w = kept("w2w", 2 * H, U8)
-        w2s = kept("w2s", H, U8)
-        tab2w = [kept(f"tab2w{a}", TB, U32) for a in range(2)]
-        tab2s = kept("tab2s", TB, U8)
-        w5w = [kept(f"w5w{a}", N, U32) for a in range(2)]
-        w5s = kept("w5s", N, U8)
-        gain_sb = kept("gain_sb", 2 * PACK, F32)
-        low_sb = kept("low_sb", N // P, F32)
-
-        for plane in (tabs, w2s, tab2s, w5s):
+        for plane in (tab_s, w2_s, tab2_s, w5_s):
             nc.vector.memset(plane[:].bitcast(I32), 0)
 
-        raw = {"w1a": []}
         nc.sync.dma_start(offs_sb[:], offs)
         nc.sync.dma_start(offs2_sb[:], offs2)
         nc.sync.dma_start(pos1_sb[:], pos1)
         nc.sync.dma_start(
-            out=gain_sb[:, 0 : 2 * PACK].rearrange("p (a t) -> p a t", t=PACK),
+            out=gain_sb[:].rearrange("p (a t) -> p a t", t=PACK),
             in_=gain.rearrange("(a p t) -> p a t", p=P, t=PACK),
         )
-        with nc.allow_non_contiguous_dma(reason="one offset a partition"):
+        for a in range(PASSES):
+            block = slice(a * 2 * PASS, (a + 1) * 2 * PASS)
+            nc.sync.dma_start(out=w2_w[:, block].bitcast(I32), in_=w2_words[0, :, block].bitcast(I32))
+        staged = {"w1a": [load_rows(f"w1_staged{u}", w1, 0, u * PIECE, PIECE) for u in range(2)]}
+        load_plane(tab_s, tab_scales)
+        load_words(tab_w, tab_words[0])
+        load_plane(w2_s, w2_scales)
+        staged["w1b"] = [load_rows(f"w1_staged{u}", w1, 0, u * PIECE, PIECE) for u in range(2, 4)]
+        for a in range(PASSES):
+            load_words(tab2_w[a], tab2_words[a])
+        staged["w3"] = [load_rows(f"w3_staged{a}", w3, a, 0, N) for a in range(PASSES)]
+        load_plane(tab2_s, tab2_scales)
+        load_plane(w5_s, w5_scales)
+        staged["w4"] = [load_rows(f"w4_staged{a}", w4, a, 0, N) for a in range(PASSES)]
+        for a in range(PASSES):
+            load_words(w5_w[a], w5_words[a])
+        with nc.allow_non_contiguous_dma(reason="low[128 n + p] is a scalar of partition p"):
             nc.sync.dma_start(out=low_sb[:], in_=low.rearrange("(n p) -> p n", p=P))
-        raw["w1a"].append(load_block("w1a_0", w1, 0, 0, PAIR)[:])
-        raw["w1a"].append(load_block("w1a_1", w1, 0, PAIR, PAIR)[:])
-        nc.sync.dma_start(out=w2w[:].bitcast(I32), in_=w2_words[0].bitcast(I32))
-        load_scales(nc.sync, tabs, tab_scales)
-        nc.sync.dma_start(out=tabw[:].bitcast(I32), in_=words_of(tab_words[0]))
-        load_scales(nc.sync, w2s, w2_scales)
-        raw["w1b"] = load_halves("w1b", w1, 0, BANK)
-        for a in range(2):
-            nc.sync.dma_start(out=tab2w[a][:].bitcast(I32), in_=words_of(tab2_words[a]))
-        raw["w3"] = [load_block(f"w3raw{a}", w3, a, 0, BANK) for a in range(2)]
-        load_scales(nc.sync, tab2s, tab2_scales)
-        load_scales(nc.sync, w5s, w5_scales)
-        raw["w4"] = [load_block(f"w4raw{a}", w4, a, 0, BANK) for a in range(2)]
-        for a in range(2):
-            nc.sync.dma_start(out=w5w[a][:].bitcast(I32), in_=words_of(w5_words[a]))
-
-        def copy_on(engine, out_ap, in_ap):
-            if engine == "scalar":
-                nc.scalar.copy(out=out_ap, in_=in_ap)
-            elif engine == "gpsimd":
-                nc.gpsimd.tensor_scalar(out=out_ap, in0=in_ap, scalar1=1.0, scalar2=0.0, op0=ALU.mult, op1=ALU.add)
-            else:
-                nc.vector.tensor_copy(out=out_ap, in_=in_ap)
 
         widths = {"w1a": BANK, "w1b": BANK, "w3": 2 * BANK, "w4": 2 * BANK, "h0": 2 * BANK, "h1": 2 * BANK}
-        rounded = {name: kept(name + "g", PACK * width, BF16) for name, width in widths.items()}
-        codes = {name: kept(name + "c", width, U32) for name, width in widths.items()}
-        scales = {name: kept(name + "s", width, U8) for name, width in widths.items()}
+        rounded = {name: kept(name + "_rounded", PACK * width, BF16) for name, width in widths.items()}
+        words = {name: kept(name + "_words", width, U32) for name, width in widths.items()}
+        planes = {name: kept(name + "_plane", width, U8) for name, width in widths.items()}
 
         def quantise(name, lo, hi):
             nc.vector.quantize_mx(
-                out=codes[name][:, lo:hi].bitcast(FP8X4), scales=scales[name][:, lo:hi],
+                out=words[name][:, lo:hi].bitcast(FP8X4), scales=planes[name][:, lo:hi],
                 in_=rounded[name][:, PACK * lo : PACK * hi],
             )
 
-        def round_plain(name, a, lo, hi, engine):
-            dst = rounded[name][:, PACK * (a * BANK + lo) : PACK * (a * BANK + hi)]
-            if engine == "gpsimd":
-                copy_on(engine, dst.rearrange("p (c j) -> p c j", j=PACK), raw[name][a][:, :, lo:hi].rearrange("p j c -> p c j"))
-                return
-            copy_on(
-                engine, dst.rearrange("p (c i j) -> p c j i", i=4, j=PACK),
-                raw[name][a][:, :, lo:hi].rearrange("p j (c i) -> p c j i", i=4),
+        def round_plain(name, a, u, copy):
+            first = a * BANK + u * PIECE
+            dst = rounded[name][:, PACK * first : PACK * (first + PIECE)]
+            src = staged[name][a][:, :, u * PIECE : (u + 1) * PIECE]
+            copy(
+                out=dst.rearrange("p (c i t) -> p c t i", i=LINE, t=PACK),
+                in_=src.rearrange("p t (c i) -> p c t i", i=LINE),
             )
 
-        def round_dealt(name, u, engine):
-            dst = rounded[name][:].rearrange("p (t m j) -> p m j t", t=PACK, j=PACK)
-            copy_on(engine, dst[:, 64 * u : 64 * (u + 1)], raw[name][u].rearrange("p j (m t) -> p m j t", t=PACK))
+        def round_dealt(name, u, copy):
+            dst = rounded[name][:].rearrange("p (j m t) -> p m t j", j=PACK, t=PACK)
+            span = PIECE // PACK
+            copy(
+                out=dst[:, u * span : (u + 1) * span],
+                in_=staged[name][u][:].rearrange("p t (m j) -> p m t j", j=PACK),
+            )
 
-        vw = [kept(f"vw{jh}", BANK, U32) for jh in range(2)]
-        vs = [kept(f"vs{jh}", BANK, U8) for jh in range(2)]
-        cuts = [offs_sb[:, jh * (BANK // 16) : (jh + 1) * (BANK // 16)] for jh in range(2)]
-        v2w = [kept(f"v2w{a}", PICK, U32) for a in range(2)]
-        v2s = kept("v2s", PICK, U8)
-        w2d = kept("w2d", 2 * H, U8)
-        w2ds = kept("w2ds", H, U8)
-        y = [kept(f"y{n}", S, F32) for n in range(N // P)]
+        v_w = [kept(f"v_w{half}", BANK, U32) for half in range(HALVES)]
+        v_s = [kept(f"v_s{half}", BANK, U8) for half in range(HALVES)]
+        list_cols = BANK // LIST_ROWS
+        cuts = [offs_sb[:, half * list_cols : (half + 1) * list_cols] for half in range(HALVES)]
+        v2_w = [kept(f"v2_w{a}", PICK, U32) for a in range(PASSES)]
+        v2_s = kept("v2_s", PICK, U8)
+        w2_dealt_w = kept("w2_dealt_w", 2 * H, U8)
+        w2_dealt_s = kept("w2_dealt_s", H, U8)
+        y = [kept(f"y{n}", S, F32) for n in range(TILES)]
 
-        steps = [(jh, a, pair) for jh in range(2) for a in range(2) for pair in range(2)]
-        banks, least, bent = {}, {}, {}
+        def gather(dst, window, offsets):
+            nc.vector.tensor_copy(dst[:], window[:].indirect(offsets))
 
-        def readings(s, u):
-            jh, a, pair = steps[s]
-            w1c, w1s = codes["w1" + "ab"[a]], scales["w1" + "ab"[a]]
-            c0 = pair * PAIR + u * CHUNK
-            cols = slice(c0, c0 + CHUNK)
-            d1 = psum.tile([P, PACK, CHUNK], F32, name="d1", bufs=2)
-            d2 = psum.tile([P, PACK, CHUNK], F32, name="d2", bufs=3)
+        def deal_w2_words():
+            nc.vector.tensor_copy(
+                out=w2_dealt_w[:].bitcast(U16).rearrange("p (a j m) -> p a j m", a=PASSES, j=PACK),
+                in_=w2_w[:].bitcast(U16).rearrange("p (a m j) -> p a j m", a=PASSES, j=PACK),
+            )
+
+        def deal_w2_scales(a):
+            block = slice(a * PASS, (a + 1) * PASS)
+            nc.vector.tensor_copy(
+                out=w2_dealt_s[:, block].rearrange("p (j m) -> p j m", j=PACK),
+                in_=w2_s[:, block].rearrange("p (m j) -> p j m", j=PACK),
+            )
+
+        steps = [(half, a, pair) for half in range(HALVES) for a in range(PASSES) for pair in range(BANK // PAIR)]
+        last = len(steps) - 1
+        readings, least, bent = {}, {}, {}
+
+        def read_patches(s, u):
+            half, a, pair = steps[s]
+            w1_name = ("w1a", "w1b")[a]
+            first = pair * PAIR + u * CHUNK
+            cols = slice(first, first + CHUNK)
+            d1 = psum.tile([P, PACK, CHUNK], F32, name="d1", tag="bank")
+            d2 = psum.tile([P, PACK, CHUNK], F32, name="d2", tag="bank")
             for t in range(PACK):
                 rows = slice(t * P, (t + 1) * P)
                 nc.tensor.matmul_mx(
-                    out=d1[:, t, :], lhsT=w1c[:, rows].bitcast(FP8X4), lhsT_scale=w1s[:, rows],
-                    rhs=vw[jh][:, cols].bitcast(FP8X4), rhs_scale=vs[jh][:, cols], start=True, stop=True,
+                    out=d1[:, t, :], lhsT=words[w1_name][:, rows].bitcast(FP8X4), lhsT_scale=planes[w1_name][:, rows],
+                    rhs=v_w[half][:, cols].bitcast(FP8X4), rhs_scale=v_s[half][:, cols], start=True, stop=True,
                 )
             for t in range(PACK):
-                r0 = a * PASS + t * P
+                row = a * PASS + t * P
                 nc.tensor.matmul_mx(
-                    out=d2[:, t, :], lhsT=w2d[:, 2 * r0 : 2 * (r0 + P)].bitcast(FP4X4),
-                    lhsT_scale=w2ds[:, r0 : r0 + P],
-                    rhs=vw[jh][:, cols].bitcast(FP8X4), rhs_scale=vs[jh][:, cols], start=True, stop=True,
+                    out=d2[:, t, :], lhsT=w2_dealt_w[:, 2 * row : 2 * (row + P)].bitcast(FP4X4),
+                    lhsT_scale=w2_dealt_s[:, row : row + P],
+                    rhs=v_w[half][:, cols].bitcast(FP8X4), rhs_scale=v_s[half][:, cols], start=True, stop=True,
                 )
             d1_sb = ring.tile([P, CHUNK, PACK], F32, name="d1_sb")
             nc.scalar.copy(out=d1_sb[:], in_=d1[:].rearrange("p t c -> p c t"))
-            banks[s, u] = (d1_sb, d2)
+            readings[s, u] = (d1_sb, d2)
 
         def take_least(s, u):
             if u == 0:
                 least[s] = ring.tile([P, PAIR, PACK], F32, name="least")
-            d1_sb, d2 = banks[s, u]
+            d1_sb, d2 = readings[s, u]
             nc.vector.tensor_tensor(
                 out=least[s][:, u * CHUNK : (u + 1) * CHUNK, :], in0=d2[:].rearrange("p t c -> p c t"),
                 in1=d1_sb[:], op=ALU.min,
             )
 
-        def bend(s, lo=0, hi=PAIR):
+        def bend(s, lo, hi):
             if lo == 0:
-                bent[s] = ring.tile([P, PAIR, PACK], F32, name="bent", bufs=3)
+                bent[s] = ring.tile([P, PAIR, PACK], F32, name="bent")
             nc.scalar.activation(out=bent[s][:, lo:hi, :], in_=least[s][:, lo:hi, :], func=ACT.Tanh)
 
-        def apply_gain(s, lo, hi, unit, gains):
-            jh, a, pair = steps[s]
-            c0 = a * BANK + pair * PAIR
-            dst = rounded[f"h{jh}"][:, PACK * (c0 + lo) : PACK * (c0 + hi)].rearrange("p (c t) -> p c t", t=PACK)
-            spread = gains[:, a * PACK : (a + 1) * PACK].unsqueeze(1).to_broadcast([P, hi - lo, PACK])
-            unit.tensor_tensor(out=dst, in0=bent[s][:, lo:hi, :], in1=spread, op=ALU.mult)
+        def apply_gain(s, lo, hi):
+            half, a, pair = steps[s]
+            first = a * BANK + pair * PAIR
+            dst = rounded[f"h{half}"][:, PACK * (first + lo) : PACK * (first + hi)]
+            gains = gain_sb[:, a * PACK : (a + 1) * PACK].unsqueeze(1).to_broadcast([P, hi - lo, PACK])
+            nc.vector.tensor_tensor(
+                out=dst.rearrange("p (c t) -> p c t", t=PACK), in0=bent[s][:, lo:hi, :], in1=gains, op=ALU.mult,
+            )
 
         def first_stage(s):
-            readings(s, 0)
-            readings(s, 1)
-            if s - 2 >= POOL_STEPS:
-                apply_gain(s - 2, 0, PAIR, nc.vector, gain_v)
+            read_patches(s, 0)
+            read_patches(s, 1)
+            if s >= 2:
+                apply_gain(s - 2, 0, PAIR)
             take_least(s, 0)
             take_least(s, 1)
             if s >= 1:
-                bend(s - 1)
-            if 0 <= s - 1 < POOL_STEPS:
-                for lo in range(0, PAIR, POOL_CUT):
-                    apply_gain(s - 1, lo, lo + POOL_CUT, nc.gpsimd, gain_sb)
+                bend(s - 1, 0, PAIR)
 
-        def own(name):
-            return [(codes[name][:, a * BANK : (a + 1) * BANK], scales[name][:, a * BANK : (a + 1) * BANK], 0) for a in range(2)]
+        def quantised(name):
+            cols = [slice(a * BANK, (a + 1) * BANK) for a in range(PASSES)]
+            return [(words[name][:, c], planes[name][:, c], 0) for c in cols]
 
-        def product(tag, bufs, lhs, rhs, n):
-            acc = psum.tile([P, BANK], F32, name=tag, bufs=bufs)
+        def product(stationary, moving, n):
+            acc = psum.tile([P, BANK], F32, name="acc", tag="bank")
             rows = slice(n * P, (n + 1) * P)
-            for a in range(2):
-                (lc, ls, lk), (rc, rs, rk) = lhs[a], rhs[a]
+            for a in range(PASSES):
+                (lhs_w, lhs_s, lhs_first), (rhs_w, rhs_s, rhs_first) = stationary[a], moving[a]
                 nc.tensor.matmul_mx(
-                    out=acc[:], lhsT=lc[:, rows].bitcast(FP8X4), lhsT_scale=ls[lk:P, rows],
-                    rhs=rc.bitcast(FP8X4), rhs_scale=rs[rk:P, :], start=(a == 0), stop=(a == 1),
+                    out=acc[:], lhsT=lhs_w[:, rows].bitcast(FP8X4), lhsT_scale=lhs_s[lhs_first:P, rows],
+                    rhs=rhs_w.bitcast(FP8X4), rhs_scale=rhs_s[rhs_first:P, :],
+                    start=(a == 0), stop=(a == PASSES - 1),
                 )
             return acc
 
-        def second_stage(jh, n):
-            acc = product("acc", 3, own("w3"), own(f"h{jh}"), n)
-            nc.scalar.copy(out=y[n][:, jh * BANK : (jh + 1) * BANK], in_=acc[:])
+        def second_stage(half):
+            for n in range(TILES):
+                acc = product(quantised("w3"), quantised(f"h{half}"), n)
+                nc.scalar.copy(out=y[n][:, half * BANK : (half + 1) * BANK], in_=acc[:])
 
-        def deal_words():
-            nc.vector.tensor_copy(
-                out=w2d[:].bitcast(U16).rearrange("p (a t m) -> p a t m", a=2, t=PACK),
-                in_=w2w[:].bitcast(U16).rearrange("p (a m t) -> p a t m", a=2, t=PACK),
-            )
+        on_scalar, on_vector = nc.scalar.copy, nc.vector.tensor_copy
 
-        def deal_scales(a):
-            cols = slice(a * PASS, (a + 1) * PASS)
-            nc.vector.tensor_copy(
-                out=w2ds[:, cols].rearrange("p (t m) -> p t m", t=PACK),
-                in_=w2s[:, cols].rearrange("p (m t) -> p t m", t=PACK),
-            )
-
-        gain_v = gain_sb
-        round_dealt("w1a", 0, "scalar")
-        round_dealt("w1a", 1, "vector")
+        round_dealt("w1a", 0, on_scalar)
+        round_dealt("w1a", 1, on_vector)
         quantise("w1a", 0, BANK)
-        deal_words()
-        for jh in range(2):
-            nc.vector.tensor_copy(vs[jh][:], tabs[:].indirect(cuts[jh]))
-        nc.vector.tensor_copy(vw[0][:], tabw[:].indirect(cuts[0]))
-        deal_scales(0)
-        nc.vector.tensor_copy(vw[1][:], tabw[:].indirect(cuts[1]))
+        deal_w2_words()
+        for half in range(HALVES):
+            gather(v_s[half], tab_s, cuts[half])
+        gather(v_w[0], tab_w, cuts[0])
+        deal_w2_scales(0)
+        gather(v_w[1], tab_w, cuts[1])
 
         first_stage(0)
-        round_dealt("w1b", 0, "scalar")
-        deal_scales(1)
-        round_dealt("w1b", 1, "vector")
+        round_dealt("w1b", 0, on_scalar)
+        deal_w2_scales(1)
+        round_dealt("w1b", 1, on_vector)
         quantise("w1b", 0, BANK)
         first_stage(1)
-        nc.vector.tensor_copy(v2w[0][:], tab2w[0][:].indirect(offs2_sb[:]))
+        gather(v2_w[0], tab2_w[0], offs2_sb[:])
         first_stage(2)
-        round_plain("w3", 0, 0 * PAIR, 1 * PAIR, "scalar")
-        nc.vector.tensor_copy(v2w[1][:], tab2w[1][:].indirect(offs2_sb[:]))
+        round_plain("w3", 0, 0, on_scalar)
+        gather(v2_w[1], tab2_w[1], offs2_sb[:])
         first_stage(3)
-        round_plain("w3", 0, 1 * PAIR, 2 * PAIR, "scalar")
+        round_plain("w3", 0, 1, on_scalar)
         quantise("h0", 0, BANK)
         first_stage(4)
-        round_plain("w3", 1, 0 * PAIR, 1 * PAIR, "scalar")
-        nc.vector.tensor_copy(v2s[:], tab2s[:].indirect(offs2_sb[:]))
+        round_plain("w3", 1, 0, on_scalar)
+        gather(v2_s, tab2_s, offs2_sb[:])
         first_stage(5)
-        round_plain("w3", 1, 1 * PAIR, 2 * PAIR, "scalar")
+        round_plain("w3", 1, 1, on_scalar)
         quantise("w3", 0, 2 * BANK)
         quantise("h0", BANK, 2 * BANK)
         first_stage(6)
-        round_plain("w4", 0, 0 * PAIR, 1 * PAIR, "vector")
-        second_stage(0, 0)
-        first_stage(7)
+        round_plain("w4", 0, 0, on_vector)
+        first_stage(last)
         quantise("h1", 0, BANK)
-        second_stage(0, 1)
-        bend(7, 0, CHUNK)
-        apply_gain(6, 0, PAIR, nc.vector, gain_v)
-        bend(7, CHUNK, PAIR)
-        apply_gain(7, 0, CHUNK, nc.vector, gain_v)
+
+        bend(last, 0, CHUNK)
+        apply_gain(last - 1, 0, PAIR)
+        bend(last, CHUNK, PAIR)
+        apply_gain(last, 0, CHUNK)
         quantise("h1", BANK, BANK + PAIR)
-        apply_gain(7, CHUNK, PAIR, nc.vector, gain_v)
+        apply_gain(last, CHUNK, PAIR)
         quantise("h1", BANK + PAIR, 2 * BANK)
-        second_stage(0, 2)
-        second_stage(0, 3)
-        round_plain("w4", 0, 1 * PAIR, 2 * PAIR, "vector")
-        for n in range(N // P):
-            second_stage(1, n)
-        round_plain("w4", 1, 0 * PAIR, 1 * PAIR, "vector")
-        round_plain("w4", 1, 1 * PAIR, 2 * PAIR, "scalar")
+
+        second_stage(0)
+        round_plain("w4", 0, 1, on_vector)
+        second_stage(1)
+        round_plain("w4", 1, 0, on_vector)
+        round_plain("w4", 1, 1, on_scalar)
         quantise("w4", 0, BANK)
         quantise("w4", BANK, 2 * BANK)
 
-        v2 = [(v2w[a][:], v2s, 4 * a) for a in range(2)]
-        w5q = [(w5w[a], w5s, 4 * a) for a in range(2)]
-        picked = [kept(f"picked{n}", PICK, F32) for n in range(N // P)]
-
-        def pick(n):
-            nc.vector.tensor_copy(picked[n][:], y[n][:].indirect(pos1_sb[:]))
-
-        def finish(n):
-            cap = product("d2", 3, own("w4"), v2, n)
-            base = product("d1", 2, w5q, v2, n)
+        v2 = [(v2_w[a][:], v2_s, PACK * a) for a in range(PASSES)]
+        w5 = [(w5_w[a], w5_s, PACK * a) for a in range(PASSES)]
+        picked = [kept(f"picked{n}", PICK, F32) for n in range(TILES)]
+        for n in range(TILES):
+            gather(picked[n], y[n], pos1_sb[:])
+        for n in range(TILES):
+            cap = product(quantised("w4"), v2, n)
+            base = product(w5, v2, n)
             capped = ring.tile([P, PICK], F32, name="capped")
             nc.vector.tensor_tensor(out=capped[:], in0=cap[:], in1=picked[n][:], op=ALU.min)
-            result = keep.tile([P, PICK], F32, name=f"result{n}", tag=f"w1{'ab'[n // 2]}_{n % 2}")
-            nc.vector.scalar_tensor_tensor(
-                out=result[:], in0=base[:], scalar=low_sb[:, n : n + 1], in1=capped[:], op0=ALU.add, op1=ALU.max,
-            )
-            nc.sync.dma_start(out=out[n * P : (n + 1) * P, :], in_=result[:])
-
-        for n in range(N // P):
-            pick(n)
-        for n in range(N // P):
-            finish(n)
+            result = keep.tile([P, PICK], F32, name=f"result{n}", tag=f"w1_staged{n}")
+            width = PICK // 2 if n == TILES - 1 else PICK
+            for lo in range(0, PICK, width):
+                cols = slice(lo, lo + width)
+                nc.vector.scalar_tensor_tensor(
+                    out=result[:, cols], in0=base[:, cols], scalar=low_sb[:, n : n + 1], in1=capped[:, cols],
+                    op0=ALU.add, op1=ALU.max,
+                )
+                nc.sync.dma_start(out=out[n * P : (n + 1) * P, cols], in_=result[:, cols])

from contextlib import ExitStack

import concourse.mybir as mybir

K, H, N, T, S, M, TB, PICK = 512, 1024, 512, 4096, 1024, 1024, 2048, 512
FLOPS = 2 * (2 * K * H * S + H * N * S + 2 * M * N * PICK)

F32 = mybir.dt.float32
BF16 = mybir.dt.bfloat16
I32 = mybir.dt.int32
U32 = mybir.dt.uint32
U16 = mybir.dt.uint16
U8 = mybir.dt.uint8
FP8X4 = mybir.dt.float8_e4m3fn_x4
FP4X4 = mybir.dt.float4_e2m1fn_x4
ALU = mybir.AluOpType
ACT = mybir.ActivationFunctionType

P = 128
PACK = 4
PASS = P * PACK
PASSES = 2
BANK = 512
BANKS = 8
HALVES = S // BANK
CHUNK = BANK // PACK
PAIR = 2 * CHUNK
PIECE = BANK // 2
LIST_ROWS = 16
LINE = 4
RING = 3
TILES = N // P


def tile_list_crystal_deposit_grading_kernel(
    tc, tab_words, tab_scales, offs, tab2_words, tab2_scales, offs2, pos1, w1, w2_words, w2_scales,
    gain, w3, w4, w5_words, w5_scales, low, out,
):
    nc = tc.nc
    with ExitStack() as ctx:
        keep = ctx.enter_context(tc.tile_pool(name="keep", bufs=1))
        ring = ctx.enter_context(tc.tile_pool(name="ring", bufs=RING))
        psum = ctx.enter_context(tc.psum_pool(name="psum", bufs=BANKS))

        def kept(name, width, dtype):
            return keep.tile([P, width], dtype, name=name, align_bytes=64)

        def load_words(tile, dram):
            nc.sync.dma_start(out=tile[:].bitcast(I32), in_=dram.rearrange("p n t -> p (n t)").bitcast(I32))

        def load_plane(plane, dram):
            passes = dram.shape[0]
            for q in range(4):
                rows = dram[:, 4 * q : 4 * q + 4, :] if passes > 1 else dram[0, 4 * q : 4 * q + 4, :]
                nc.sync.dma_start(out=plane[32 * q : 32 * q + 4 * passes, :].bitcast(I32), in_=rows.bitcast(I32))

        def load_rows(name, w, a, first, width):
            staged = keep.tile([P, PACK, width], F32, name=name, tag=name)
            rows = w[a * PASS : (a + 1) * PASS, first : first + width]
            nc.sync.dma_start(out=staged[:], in_=rows.rearrange("(p t) c -> p t c", t=PACK))
            return staged

        offs_sb = keep.tile([P, S // LIST_ROWS], U16, name="offs_sb")
        offs2_sb = keep.tile([P, PICK // LIST_ROWS], U16, name="offs2_sb")
        pos1_sb = keep.tile([P, PICK // LIST_ROWS], U16, name="pos1_sb")
        tab_w = kept("tab_w", T, U32)
        tab_s = kept("tab_s", T, U8)
        w2_w = kept("w2_w", 2 * H, U8)
        w2_s = kept("w2_s", H, U8)
        tab2_w = [kept(f"tab2_w{a}", TB, U32) for a in range(PASSES)]
        tab2_s = kept("tab2_s", TB, U8)
        w5_w = [kept(f"w5_w{a}", N, U32) for a in range(PASSES)]
        w5_s = kept("w5_s", N, U8)
        gain_sb = kept("gain_sb", PASSES * PACK, F32)
        low_sb = kept("low_sb", TILES, F32)

        for plane in (tab_s, w2_s, tab2_s, w5_s):
            nc.vector.memset(plane[:].bitcast(I32), 0)

        nc.sync.dma_start(offs_sb[:], offs)
        nc.sync.dma_start(offs2_sb[:], offs2)
        nc.sync.dma_start(pos1_sb[:], pos1)
        nc.sync.dma_start(
            out=gain_sb[:].rearrange("p (a t) -> p a t", t=PACK),
            in_=gain.rearrange("(a p t) -> p a t", p=P, t=PACK),
        )
        for a in range(PASSES):
            block = slice(a * 2 * PASS, (a + 1) * 2 * PASS)
            nc.sync.dma_start(out=w2_w[:, block].bitcast(I32), in_=w2_words[0, :, block].bitcast(I32))
        staged = {"w1a": [load_rows(f"w1_staged{u}", w1, 0, u * PIECE, PIECE) for u in range(2)]}
        load_plane(tab_s, tab_scales)
        load_words(tab_w, tab_words[0])
        load_plane(w2_s, w2_scales)
        staged["w1b"] = [load_rows(f"w1_staged{u}", w1, 0, u * PIECE, PIECE) for u in range(2, 4)]
        for a in range(PASSES):
            load_words(tab2_w[a], tab2_words[a])
        staged["w3"] = [load_rows(f"w3_staged{a}", w3, a, 0, N) for a in range(PASSES)]
        load_plane(tab2_s, tab2_scales)
        load_plane(w5_s, w5_scales)
        staged["w4"] = [load_rows(f"w4_staged{a}", w4, a, 0, N) for a in range(PASSES)]
        for a in range(PASSES):
            load_words(w5_w[a], w5_words[a])
        with nc.allow_non_contiguous_dma(reason="low[128 n + p] is a scalar of partition p"):
            nc.sync.dma_start(out=low_sb[:], in_=low.rearrange("(n p) -> p n", p=P))

        widths = {"w1a": BANK, "w1b": BANK, "w3": 2 * BANK, "w4": 2 * BANK, "h0": 2 * BANK, "h1": 2 * BANK}
        rounded = {name: kept(name + "_rounded", PACK * width, BF16) for name, width in widths.items()}
        words = {name: kept(name + "_words", width, U32) for name, width in widths.items()}
        planes = {name: kept(name + "_plane", width, U8) for name, width in widths.items()}

        def quantise(name, lo, hi):
            nc.vector.quantize_mx(
                out=words[name][:, lo:hi].bitcast(FP8X4), scales=planes[name][:, lo:hi],
                in_=rounded[name][:, PACK * lo : PACK * hi],
            )

        def round_plain(name, a, u, copy):
            first = a * BANK + u * PIECE
            dst = rounded[name][:, PACK * first : PACK * (first + PIECE)]
            src = staged[name][a][:, :, u * PIECE : (u + 1) * PIECE]
            copy(
                out=dst.rearrange("p (c i t) -> p c t i", i=LINE, t=PACK),
                in_=src.rearrange("p t (c i) -> p c t i", i=LINE),
            )

        def round_dealt(name, u, copy):
            dst = rounded[name][:].rearrange("p (j m t) -> p m t j", j=PACK, t=PACK)
            span = PIECE // PACK
            copy(
                out=dst[:, u * span : (u + 1) * span],
                in_=staged[name][u][:].rearrange("p t (m j) -> p m t j", j=PACK),
            )

        v_w = [kept(f"v_w{half}", BANK, U32) for half in range(HALVES)]
        v_s = [kept(f"v_s{half}", BANK, U8) for half in range(HALVES)]
        list_cols = BANK // LIST_ROWS
        cuts = [offs_sb[:, half * list_cols : (half + 1) * list_cols] for half in range(HALVES)]
        v2_w = [kept(f"v2_w{a}", PICK, U32) for a in range(PASSES)]
        v2_s = kept("v2_s", PICK, U8)
        w2_dealt_w = kept("w2_dealt_w", 2 * H, U8)
        w2_dealt_s = kept("w2_dealt_s", H, U8)
        y = [kept(f"y{n}", S, F32) for n in range(TILES)]

        def gather(dst, window, offsets):
            nc.vector.tensor_copy(dst[:], window[:].indirect(offsets))

        def deal_w2_words():
            nc.vector.tensor_copy(
                out=w2_dealt_w[:].bitcast(U16).rearrange("p (a j m) -> p a j m", a=PASSES, j=PACK),
                in_=w2_w[:].bitcast(U16).rearrange("p (a m j) -> p a j m", a=PASSES, j=PACK),
            )

        def deal_w2_scales(a):
            block = slice(a * PASS, (a + 1) * PASS)
            nc.vector.tensor_copy(
                out=w2_dealt_s[:, block].rearrange("p (j m) -> p j m", j=PACK),
                in_=w2_s[:, block].rearrange("p (m j) -> p j m", j=PACK),
            )

        steps = [(half, a, pair) for half in range(HALVES) for a in range(PASSES) for pair in range(BANK // PAIR)]
        last = len(steps) - 1
        readings, least, bent = {}, {}, {}

        def read_patches(s, u):
            half, a, pair = steps[s]
            w1_name = ("w1a", "w1b")[a]
            first = pair * PAIR + u * CHUNK
            cols = slice(first, first + CHUNK)
            d1 = psum.tile([P, PACK, CHUNK], F32, name="d1", tag="bank")
            d2 = psum.tile([P, PACK, CHUNK], F32, name="d2", tag="bank")
            for t in range(PACK):
                rows = slice(t * P, (t + 1) * P)
                nc.tensor.matmul_mx(
                    out=d1[:, t, :], lhsT=words[w1_name][:, rows].bitcast(FP8X4), lhsT_scale=planes[w1_name][:, rows],
                    rhs=v_w[half][:, cols].bitcast(FP8X4), rhs_scale=v_s[half][:, cols], start=True, stop=True,
                )
            for t in range(PACK):
                row = a * PASS + t * P
                nc.tensor.matmul_mx(
                    out=d2[:, t, :], lhsT=w2_dealt_w[:, 2 * row : 2 * (row + P)].bitcast(FP4X4),
                    lhsT_scale=w2_dealt_s[:, row : row + P],
                    rhs=v_w[half][:, cols].bitcast(FP8X4), rhs_scale=v_s[half][:, cols], start=True, stop=True,
                )
            d1_sb = ring.tile([P, CHUNK, PACK], F32, name="d1_sb")
            nc.scalar.copy(out=d1_sb[:], in_=d1[:].rearrange("p t c -> p c t"))
            readings[s, u] = (d1_sb, d2)

        def take_least(s, u):
            if u == 0:
                least[s] = ring.tile([P, PAIR, PACK], F32, name="least")
            d1_sb, d2 = readings[s, u]
            nc.vector.tensor_tensor(
                out=least[s][:, u * CHUNK : (u + 1) * CHUNK, :], in0=d2[:].rearrange("p t c -> p c t"),
                in1=d1_sb[:], op=ALU.min,
            )

        def bend(s, lo, hi):
            if lo == 0:
                bent[s] = ring.tile([P, PAIR, PACK], F32, name="bent")
            nc.scalar.activation(out=bent[s][:, lo:hi, :], in_=least[s][:, lo:hi, :], func=ACT.Tanh)

        def apply_gain(s, lo, hi):
            half, a, pair = steps[s]
            first = a * BANK + pair * PAIR
            dst = rounded[f"h{half}"][:, PACK * (first + lo) : PACK * (first + hi)]
            gains = gain_sb[:, a * PACK : (a + 1) * PACK].unsqueeze(1).to_broadcast([P, hi - lo, PACK])
            nc.vector.tensor_tensor(
                out=dst.rearrange("p (c t) -> p c t", t=PACK), in0=bent[s][:, lo:hi, :], in1=gains, op=ALU.mult,
            )

        def first_stage(s):
            read_patches(s, 0)
            read_patches(s, 1)
            if s >= 2:
                apply_gain(s - 2, 0, PAIR)
            take_least(s, 0)
            take_least(s, 1)
            if s >= 1:
                bend(s - 1, 0, PAIR)

        def quantised(name):
            cols = [slice(a * BANK, (a + 1) * BANK) for a in range(PASSES)]
            return [(words[name][:, c], planes[name][:, c], 0) for c in cols]

        def product(stationary, moving, n):
            acc = psum.tile([P, BANK], F32, name="acc", tag="bank")
            rows = slice(n * P, (n + 1) * P)
            for a in range(PASSES):
                (lhs_w, lhs_s, lhs_first), (rhs_w, rhs_s, rhs_first) = stationary[a], moving[a]
                nc.tensor.matmul_mx(
                    out=acc[:], lhsT=lhs_w[:, rows].bitcast(FP8X4), lhsT_scale=lhs_s[lhs_first:P, rows],
                    rhs=rhs_w.bitcast(FP8X4), rhs_scale=rhs_s[rhs_first:P, :],
                    start=(a == 0), stop=(a == PASSES - 1),
                )
            return acc

        def second_stage(half):
            for n in range(TILES):
                acc = product(quantised("w3"), quantised(f"h{half}"), n)
                nc.scalar.copy(out=y[n][:, half * BANK : (half + 1) * BANK], in_=acc[:])

        on_scalar, on_vector = nc.scalar.copy, nc.vector.tensor_copy

        round_dealt("w1a", 0, on_scalar)
        round_dealt("w1a", 1, on_vector)
        quantise("w1a", 0, BANK)
        deal_w2_words()
        for half in range(HALVES):
            gather(v_s[half], tab_s, cuts[half])
        gather(v_w[0], tab_w, cuts[0])
        deal_w2_scales(0)
        gather(v_w[1], tab_w, cuts[1])

        first_stage(0)
        round_dealt("w1b", 0, on_scalar)
        deal_w2_scales(1)
        round_dealt("w1b", 1, on_vector)
        quantise("w1b", 0, BANK)
        first_stage(1)
        gather(v2_w[0], tab2_w[0], offs2_sb[:])
        first_stage(2)
        round_plain("w3", 0, 0, on_scalar)
        gather(v2_w[1], tab2_w[1], offs2_sb[:])
        first_stage(3)
        round_plain("w3", 0, 1, on_scalar)
        quantise("h0", 0, BANK)
        first_stage(4)
        round_plain("w3", 1, 0, on_scalar)
        gather(v2_s, tab2_s, offs2_sb[:])
        first_stage(5)
        round_plain("w3", 1, 1, on_scalar)
        quantise("w3", 0, 2 * BANK)
        quantise("h0", BANK, 2 * BANK)
        first_stage(6)
        round_plain("w4", 0, 0, on_vector)
        first_stage(last)
        quantise("h1", 0, BANK)

        bend(last, 0, CHUNK)
        apply_gain(last - 1, 0, PAIR)
        bend(last, CHUNK, PAIR)
        apply_gain(last, 0, CHUNK)
        quantise("h1", BANK, BANK + PAIR)
        apply_gain(last, CHUNK, PAIR)
        quantise("h1", BANK + PAIR, 2 * BANK)

        second_stage(0)
        round_plain("w4", 0, 1, on_vector)
        second_stage(1)
        round_plain("w4", 1, 0, on_vector)
        round_plain("w4", 1, 1, on_scalar)
        quantise("w4", 0, BANK)
        quantise("w4", BANK, 2 * BANK)

        v2 = [(v2_w[a][:], v2_s, PACK * a) for a in range(PASSES)]
        w5 = [(w5_w[a], w5_s, PACK * a) for a in range(PASSES)]
        picked = [kept(f"picked{n}", PICK, F32) for n in range(TILES)]
        for n in range(TILES):
            gather(picked[n], y[n], pos1_sb[:])
        for n in range(TILES):
            cap = product(quantised("w4"), v2, n)
            base = product(w5, v2, n)
            capped = ring.tile([P, PICK], F32, name="capped")
            nc.vector.tensor_tensor(out=capped[:], in0=cap[:], in1=picked[n][:], op=ALU.min)
            result = keep.tile([P, PICK], F32, name=f"result{n}", tag=f"w1_staged{n}")
            width = PICK // 2 if n == TILES - 1 else PICK
            for lo in range(0, PICK, width):
                cols = slice(lo, lo + width)
                nc.vector.scalar_tensor_tensor(
                    out=result[:, cols], in0=base[:, cols], scalar=low_sb[:, n : n + 1], in1=capped[:, cols],
                    op0=ALU.add, op1=ALU.max,
                )
                nc.sync.dma_start(out=out[n * P : (n + 1) * P, cols], in_=result[:, cols])
